import numpy as np
import ml_dtypes


def mxq(x, axis, fmt="e4m3"):
    dtype, down = {"e4m3": (ml_dtypes.float8_e4m3fn, 7), "e5m2": (ml_dtypes.float8_e5m2, 14)}[fmt]
    v = np.moveaxis(np.asarray(x, np.float32).astype(ml_dtypes.bfloat16).astype(np.float64), axis, -1)
    blocks = v.reshape(v.shape[:-1] + (-1, 32))
    amax = np.abs(blocks).max(-1, keepdims=True)
    byte = np.maximum(np.where(amax > 0, np.frexp(amax)[1] - 1 + 127, 0) - down, 1)
    scale = np.exp2(byte - 127.0)
    codes = (blocks / scale).astype(np.float32).astype(dtype).astype(np.float64)
    return np.moveaxis((codes * scale).reshape(v.shape), -1, axis)


WIDE = False


def mx_kscale(k):
    if not WIDE:
        return np.ones(k)
    levels = np.array([10, -10, 5, -5, 0])
    if k % 512:
        return np.exp2(np.random.permutation(np.resize(levels, k // 32))).repeat(32)
    a = np.empty((k // 512, 16))
    for p in range(k // 512):
        a[p, :8] = np.random.permutation(np.resize(levels, 8))
        for g in range(8):
            far = levels[np.abs(levels - a[p, g]) >= 10]
            a[p, g + 8] = far[np.random.randint(len(far))]
    return np.exp2(a.ravel()).repeat(32)


def f64(x):
    return np.asarray(x).astype(np.float64)


def striped(idx):
    return np.tile(np.asarray(idx).reshape(-1, 16).T, (8, 1)).astype(np.uint16)


def unstriped(offs):
    return offs[:16].T.reshape(-1).astype(np.int64)


def striped8(idx):
    return np.asarray(idx).reshape(8, -1, 16).transpose(0, 2, 1).reshape(128, -1).astype(np.uint16)


def unstriped8(offs):
    return offs.reshape(8, 16, -1).transpose(0, 2, 1).reshape(8, -1).astype(np.int64)


def pick8(x, idx, run):
    r = np.arange(len(x))
    return x[r[:, None], idx[r % (8 * run) // run]]


E2M1 = np.array([0.0, 0.5, 1.0, 1.5, 2.0, 3.0, 4.0, 6.0, -0.0, -0.5, -1.0, -1.5, -2.0, -3.0, -4.0, -6.0])


def pack_weight(w, fmt):
    k, n = w.shape
    w = f64(np.asarray(w, np.float32).astype(ml_dtypes.bfloat16)).reshape(k // 32, 32, n)
    amax = np.abs(w).max(1)
    if fmt == "e4m3":
        byte = np.frexp(amax)[1] - 1 + 127 - 7
    else:
        mant, ex = np.frexp(amax / 6.0)
        byte = np.where(mant > 0.5, ex, ex - 1) + 127
    byte = np.clip(np.where(amax > 0, byte, 1), 1, 254)
    scaled = (w * np.exp2(127.0 - byte)[:, None, :]).reshape(k, n).astype(np.float32)
    by_word = np.ascontiguousarray(scaled.reshape(k // 512, 128, 4, n).transpose(0, 1, 3, 2))
    if fmt == "e4m3":
        words = by_word.astype(ml_dtypes.float8_e4m3fn).view(np.uint8)
    else:
        c = by_word.astype(ml_dtypes.float4_e2m1fn).view(np.uint8) & 0xF
        words = (c[..., 0::2] | (c[..., 1::2] << 4)).reshape(k // 512, 128, 2 * n)
    return np.ascontiguousarray(words), np.ascontiguousarray(byte.astype(np.uint8).reshape(k // 512, 16, n))


def unpack_weight(words, scales, fmt):
    g, _, n = scales.shape
    words = np.ascontiguousarray(words).reshape(g, 128, n, -1)
    if fmt == "e4m3":
        vals = words.view(ml_dtypes.float8_e4m3fn).astype(np.float64)
    else:
        nib = np.empty((g, 128, n, 4), np.uint8)
        nib[..., 0::2] = words & 0xF
        nib[..., 1::2] = words >> 4
        vals = E2M1[nib]
    vals = vals * np.repeat(np.exp2(scales.astype(np.float64) - 127.0), 8, axis=1)[..., None]
    return vals.transpose(0, 1, 3, 2).reshape(g * 512, n)


K, J, R, T, F, Z, M, C, O, N, S = 512, 512, 512, 2048, 2048, 512, 1024, 1024, 256, 256, 1024


def setup_inputs():
    n = np.random.standard_normal
    idx = np.random.permutation(T)[:J]
    idx2 = np.stack([np.random.permutation(F)[:R] for _ in range(8)])
    idx3 = np.random.permutation(M)[:J]
    idx4 = np.random.permutation(C)[:J]
    idx5 = np.random.permutation(C)[:O]
    idx6 = np.stack([np.random.permutation(C)[:O] for _ in range(8)])
    idx7 = np.random.permutation(S)[:N]
    fk = mx_kscale(K)
    fz = mx_kscale(Z)
    fr = mx_kscale(R)
    xtp = pack_weight(n((K, T)) * fk[:, None], "e2m1")
    xop = pack_weight(n((Z, M)) / fz[:, None], "e4m3")
    w2p = pack_weight(n((Z, R)) * 1 / np.sqrt(Z) * fz[:, None], "e2m1")
    vsp = pack_weight(n((R, S)) * 1 / np.sqrt(R) / fr[:, None], "e2m1")
    return {
        "xt_words": xtp[0],
        "xt_scales": xtp[1],
        "ua": (np.random.randint(-7, 8, (K, F)).astype(np.float64)).astype(np.float32),
        "ha": ((np.random.randint(8, 25, (K, 1)) / 1024.0) / fk[:, None]).astype(np.float32),
        "xo_words": xop[0],
        "xo_scales": xop[1],
        "w2_words": w2p[0],
        "w2_scales": w2p[1],
        "sa": (np.random.uniform(0.5, 1.6, (R, 1)) * fr[:, None]).astype(np.float32),
        "sb": (np.random.uniform(0.5, 1.6, (R, 1)) * fr[:, None]).astype(np.float32),
        "vs_words": vsp[0],
        "vs_scales": vsp[1],
        "offs": striped(idx),
        "offs2": striped8(idx2),
        "offs3": striped(idx3),
        "offs4": striped(idx4),
        "offs5": striped(idx5),
        "offs6": striped8(idx6),
        "offs7": striped(idx7),
    }


def reference(xt_words, xt_scales, ua, ha, xo_words, xo_scales, w2_words, w2_scales, sa, sb, vs_words, vs_scales, offs, offs2, offs3, offs4, offs5, offs6, offs7):
    idx = unstriped(offs)
    idx2 = unstriped8(offs2)
    idx3 = unstriped(offs3)
    idx4 = unstriped(offs4)
    idx5 = unstriped(offs5)
    idx6 = unstriped8(offs6)
    idx7 = unstriped(offs7)
    xtu = unpack_weight(xt_words, xt_scales, "e2m1")
    xou = unpack_weight(xo_words, xo_scales, "e4m3")
    w2u = unpack_weight(w2_words, w2_scales, "e2m1")
    vsu = unpack_weight(vs_words, vs_scales, "e2m1")
    wc = pick8(f64(ua), idx2, 64) * f64(ha)
    wcq = mxq(wc, 0, "e4m3")
    xtidxg = xtu[:, idx]
    xoidx3g = xou[:, idx3]
    a = wcq.T @ xtidxg + w2u.T @ xoidx3g
    pw = np.zeros((R, C))
    pw[:, idx4] = a
    hid = np.maximum(pw[:, idx5] * f64(sa), pick8(pw, idx6, 64) * f64(sb))
    vsidx7g = vsu[:, idx7]
    hidq = mxq(hid, 0, "e4m3")
    y = vsidx7g.T @ hidq
    return y

@@ -1,0 +1,211 @@
+from contextlib import ExitStack
+
+import concourse.mybir as mybir
+
+K, J, R, T, F, Z, M, C, O, N, S = 512, 512, 512, 2048, 2048, 512, 1024, 1024, 256, 256, 1024
+FLOPS = 2 * K * R * J + 2 * Z * R * J + 2 * R * N * O
+
+F32 = mybir.dt.float32
+BF16 = mybir.dt.bfloat16
+I32 = mybir.dt.int32
+U32 = mybir.dt.uint32
+U16 = mybir.dt.uint16
+U8 = mybir.dt.uint8
+FP8X4 = mybir.dt.float8_e4m3fn_x4
+FP4X4 = mybir.dt.float4_e2m1fn_x4
+COPY = mybir.ActivationFunctionType.Copy
+MAX = mybir.AluOpType.max
+
+P = 128
+PACK = 4
+LIST_ROWS = 16
+
+
+def tile_picked_tokens_codes_bank_boardmixed_store_plain_kernel(
+    tc, xt_words, xt_scales, ua, ha, xo_words, xo_scales, w2_words, w2_scales, sa, sb, vs_words, vs_scales,
+    offs, offs2, offs3, offs4, offs5, offs6, offs7, out,
+):
+    nc = tc.nc
+    with ExitStack() as ctx:
+        lists = ctx.enter_context(tc.tile_pool(name="lists", bufs=1))
+        keep = ctx.enter_context(tc.tile_pool(name="keep", bufs=1))
+        psum = ctx.enter_context(tc.psum_pool(name="psum", bufs=1))
+
+        def load_list(name, src):
+            tile = lists.tile([P, src.shape[1]], U16, name=name)
+            nc.sync.dma_start(tile[:], src)
+            return tile
+
+        def load_words(name, src, dtype, width):
+            tile = keep.tile([P, width], dtype, name=name, align_bytes=64)
+            nc.sync.dma_start(tile[:].bitcast(I32), src.bitcast(I32))
+            return tile
+
+        def scale_tile(name, width):
+            tile = keep.tile([P, width], U8, name=name, align_bytes=64)
+            nc.vector.memset(tile[:].bitcast(I32), 0)
+            return tile
+
+        def load_scales(tile, src, quadrants):
+            for q in quadrants:
+                nc.sync.dma_start(tile[32 * q : 32 * q + 4, :].bitcast(I32), src[0, 4 * q : 4 * q + 4, :].bitcast(I32))
+
+        def load_column(name, src):
+            tile = keep.tile([P, PACK], F32, name=name)
+            nc.gpsimd.dma_start(tile[:], src.rearrange("(p t) o -> p (t o)", t=PACK))
+            return tile
+
+        def gather(name, window, offsets, dtype, count):
+            tile = keep.tile([P, count], dtype, name=name, align_bytes=64)
+            nc.vector.tensor_copy(tile[:], window[:].indirect(offsets[:]))
+            return tile
+
+        xo_s = scale_tile("xo_s", M)
+        xt_s = scale_tile("xt_s", T)
+        w2_s = scale_tile("w2_s", R)
+        vs_s = scale_tile("vs_s", S)
+        ha_t = load_column("ha_t", ha)
+        sa_t = load_column("sa_t", sa)
+        sb_t = load_column("sb_t", sb)
+        ua_rows = ua.rearrange("(p t) f -> t p f", t=PACK)
+        ua_t = [keep.tile([P, F], F32, name="ua_%d" % t) for t in range(PACK)]
+
+        xo_w = load_words("xo_w", xo_words[0].rearrange("p c t -> p (c t)"), U32, M)
+        xo_list = load_list("xo_list", offs3)
+        load_scales(xo_s, xo_scales, (0, 1, 2))
+        nc.sync.dma_start(ua_t[0][:], ua_rows[0])
+        load_scales(xo_s, xo_scales, (3,))
+        xt_list = load_list("xt_list", offs)
+        ua_list = load_list("ua_list", offs2)
+        xt_w = load_words("xt_w", xt_words[0], U16, T)
+        w2_w = load_words("w2_w", w2_words[0], U16, R)
+        load_scales(xt_s, xt_scales, (0, 1))
+        nc.sync.dma_start(ua_t[1][:], ua_rows[1])
+        load_scales(xt_s, xt_scales, (2, 3))
+        load_scales(w2_s, w2_scales, (0,))
+        nc.sync.dma_start(ua_t[2][:], ua_rows[2])
+        load_scales(w2_s, w2_scales, (1, 2, 3))
+        nc.sync.dma_start(ua_t[3][:], ua_rows[3])
+        put_list = load_list("put_list", offs4)
+        vs_w = load_words("vs_w", vs_words[0], U16, S)
+        vs_list = load_list("vs_list", offs7)
+        load_scales(vs_s, vs_scales, (0, 1, 2, 3))
+        sb_list = load_list("sb_list", offs6)
+        sa_list = load_list("sa_list", offs5)
+
+        board = []
+        for t in range(PACK):
+            tile = keep.tile([P, C], F32, name="board_%d" % t)
+            nc.vector.memset(tile[:], 0.0)
+            board.append(tile)
+
+        xo_gw = gather("xo_gw", xo_w, xo_list, U32, J)
+        xo_gs = gather("xo_gs", xo_s, xo_list, U8, J)
+        xt_gw = gather("xt_gw", xt_w, xt_list, U16, J)
+        xt_gs = gather("xt_gs", xt_s, xt_list, U8, J)
+
+        w2_dw = keep.tile([P, R], U16, name="w2_dw", align_bytes=64)
+        w2_ds = keep.tile([P, R], U8, name="w2_ds", align_bytes=64)
+        nc.scalar.copy(w2_dw[:].rearrange("p (t m) -> p t m", t=PACK), w2_w[:].rearrange("p (m t) -> p t m", t=PACK))
+        nc.vector.tensor_copy(w2_ds[:].rearrange("p (t m) -> p t m", t=PACK), w2_s[:].rearrange("p (m t) -> p t m", t=PACK))
+
+        parts = [(0, 0, J // 2), (0, J // 2, J // 2)] + [(t, 0, J) for t in range(1, PACK)]
+        acc = [psum.tile([P, n], F32, name="acc_%d" % i) for i, (t, j0, n) in enumerate(parts)]
+        for i, (t, j0, n) in enumerate(parts):
+            cols = slice(P * t, P * (t + 1))
+            nc.tensor.matmul_mx(acc[i][:], lhsT=w2_dw[:, cols].bitcast(FP4X4), lhsT_scale=w2_ds[:, cols],
+                                rhs=xo_gw[:, j0 : j0 + n].bitcast(FP8X4), rhs_scale=xo_gs[:, j0 : j0 + n],
+                                start=True, stop=False)
+
+        wc_pair = [keep.tile([P, 2, R], BF16, name="wc_pair_%d" % u) for u in range(2)]
+        for j in range(PACK):
+            nc.scalar.activation(wc_pair[j // 2][:, j % 2, :], ua_t[j][:].indirect(ua_list[:]), COPY, scale=ha_t[:, j : j + 1])
+        wc_grp = [keep.tile([P, P, PACK], BF16, name="wc_grp_%d" % t, align_bytes=64) for t in range(PACK)]
+        wc_w = [keep.tile([P, P], U32, name="wc_w_%d" % t, align_bytes=64) for t in range(PACK)]
+        wc_s = [keep.tile([P, P], U8, name="wc_s_%d" % t, align_bytes=64) for t in range(PACK)]
+        dealt = [wc_pair[u][:].rearrange("p j (m t) -> p t m j", t=PACK) for u in range(2)]
+        for t in range(PACK):
+            nc.vector.tensor_copy(wc_grp[t][:, :, 0:2], dealt[0][:, t])
+        for t in range(2):
+            nc.vector.tensor_copy(wc_grp[t][:, :, 2:4], dealt[1][:, t])
+        for t in range(2, PACK):
+            nc.scalar.copy(wc_grp[t][:, :, 2:4], dealt[1][:, t])
+        for t in range(PACK):
+            nc.vector.quantize_mx(wc_w[t][:].bitcast(FP8X4), wc_s[t][:], wc_grp[t][:].rearrange("p m j -> p (m j)"))
+        for i, (t, j0, n) in enumerate(parts):
+            nc.tensor.matmul_mx(acc[i][:], lhsT=wc_w[t][:].bitcast(FP8X4), lhsT_scale=wc_s[t][:],
+                                rhs=xt_gw[:, j0 : j0 + n].bitcast(FP4X4), rhs_scale=xt_gs[:, j0 : j0 + n],
+                                start=False, stop=True)
+
+        vs_gw = keep.tile([P, N], U16, name="vs_gw", tag="wc_grp_3", align_bytes=64)
+        nc.vector.tensor_copy(vs_gw[:], vs_w[:].indirect(vs_list[:]))
+
+        hidden = [keep.tile([P, n], F32, name="hidden_%d" % i, align_bytes=64) for i, (t, j0, n) in enumerate(parts)]
+
+        def leave(i):
+            nc.scalar.copy(hidden[i][:], acc[i][:])
+
+        def put(engine, i, first, count):
+            t, j0, n = parts[i]
+            window = board[t][:].indirect(put_list[:, (j0 + first) // LIST_ROWS : (j0 + first + count) // LIST_ROWS])
+            if engine == "vector":
+                nc.vector.tensor_copy(window, hidden[i][:, first : first + count])
+            else:
+                nc.scalar.activation(window, hidden[i][:, first : first + count], COPY)
+
+        SHARE = 128
+        for i in range(4):
+            leave(i)
+        put("vector", 0, 0, J // 2)
+        put("vector", 1, 0, J // 2)
+        put("scalar", 2, 0, J // 2)
+        put("scalar", 2, J // 2, J // 2)
+        put("vector", 3, 0, J)
+        leave(4)
+        put("scalar", 4, 0, SHARE)
+        put("vector", 4, SHARE, J - SHARE)
+
+        H = O // 2
+        early = keep.tile([P, 2, 2, O], F32, name="early", tag="hidden_2", align_bytes=64)
+        late_sb = keep.tile([P, 2, O], F32, name="late_sb")
+        late_sa = [keep.tile([P, 2, H], F32, name="late_sa_%d" % h) for h in range(2)]
+        hid_grp = [keep.tile([P, H, PACK], BF16, name="hid_grp_%d" % h, align_bytes=64) for h in range(2)]
+
+        def fetch(dst, t, offsets, weight):
+            nc.scalar.activation(dst, board[t][:].indirect(offsets), COPY, scale=weight[:, t : t + 1])
+
+        def larger(h, pair, by_sa, by_sb):
+            nc.vector.tensor_tensor(hid_grp[h][:, :, 2 * pair : 2 * pair + 2], by_sa.rearrange("p t o -> p o t"),
+                                    by_sb.rearrange("p t o -> p o t"), MAX)
+
+        for t in (1, 0):
+            fetch(early[:, 0, t, :], t, sa_list[:], sa_t)
+            fetch(early[:, 1, t, :], t, sb_list[:], sb_t)
+        for h in range(2):
+            larger(h, 0, early[:, 0, :, h * H : (h + 1) * H], early[:, 1, :, h * H : (h + 1) * H])
+        vs_gs = keep.tile([P, N], U8, name="vs_gs", tag="hidden_4", align_bytes=64)
+        nc.vector.tensor_copy(vs_gs[:], vs_s[:].indirect(vs_list[:]))
+        for t in (2, 3):
+            fetch(late_sb[:, t - 2, :], t, sb_list[:], sb_t)
+            for h in range(2):
+                fetch(late_sa[h][:, t - 2, :], t, sa_list[:, h * H // LIST_ROWS : (h + 1) * H // LIST_ROWS], sa_t)
+        for h in range(2):
+            larger(h, 1, late_sa[h][:], late_sb[:, :, h * H : (h + 1) * H])
+
+        out_rows = out.rearrange("(u p) o -> p u o", p=P)
+        for h in range(2):
+            hid_w = keep.tile([P, H], U32, name="hid_w_%d" % h, align_bytes=64)
+            hid_s = keep.tile([P, H], U8, name="hid_s_%d" % h, align_bytes=64)
+            nc.vector.quantize_mx(hid_w[:].bitcast(FP8X4), hid_s[:], hid_grp[h][:].rearrange("p o t -> p (o t)"))
+            res = psum.tile([P, N // P, H], F32, name="res_%d" % h)
+            for u in range(N // P):
+                cols = slice(P * u, P * (u + 1))
+                nc.tensor.matmul_mx(res[:, u, :], lhsT=vs_gw[:, cols].bitcast(FP4X4), lhsT_scale=vs_gs[:, cols],
+                                    rhs=hid_w[:].bitcast(FP8X4), rhs_scale=hid_s[:], start=True, stop=True)
+            staged = keep.tile([P, N // P, H], F32, name="staged_%d" % h)
+            if h == 0:
+                nc.scalar.copy(staged[:], res[:])
+                nc.scalar.dma_start(out_rows[:, :, h * H : (h + 1) * H], staged[:])
+            else:
+                nc.vector.tensor_copy(staged[:], res[:])
+                nc.sync.dma_start(out_rows[:, :, h * H : (h + 1) * H], staged[:])

@@ -48,11 +48,23 @@ def tile_picked_tokens_codes_bank_boardmixed_store_plain_kernel(
 
         def load_scales(tile, src, quadrants):
             for q in quadrants:
-                nc.sync.dma_start(tile[32 * q : 32 * q + 4, :].bitcast(I32), src[0, 4 * q : 4 * q + 4, :].bitcast(I32))
+                nc.sync.dma_start(tile[q:P:32, :].bitcast(I32), src[0, q:16:4, :].bitcast(I32))
 
-        def load_column(name, src):
+        def load_staged(name, src, width):
+            tile = keep.tile([P, 2, width // 4], I32, name=name)
+            rows = src[0].bitcast(I32).rearrange("(h q i) w -> h i q w", h=2, q=2)
+            for h in range(2):
+                nc.scalar.dma_start(tile[64 * h : 64 * h + 4], rows[h])
+            return tile
+
+        def spread(tile, staged):
+            for q in range(4):
+                h = q // 2
+                nc.vector.tensor_copy(tile[32 * q : 32 * q + 4, :].bitcast(I32), staged[64 * h : 64 * h + 4, q % 2, :])
+
+        def load_column(name, src, queue):
             tile = keep.tile([P, PACK], F32, name=name)
-            nc.gpsimd.dma_start(tile[:], src.rearrange("(p t) o -> p (t o)", t=PACK))
+            queue.dma_start(tile[:], src.rearrange("(p t) o -> p (t o)", t=PACK))
             return tile
 
         def gather(name, window, offsets, dtype, count):
@@ -60,38 +72,35 @@ def tile_picked_tokens_codes_bank_boardmixed_store_plain_kernel(
             nc.vector.tensor_copy(tile[:], window[:].indirect(offsets[:]))
             return tile
 
-        xo_s = scale_tile("xo_s", M)
         xt_s = scale_tile("xt_s", T)
+        xo_s = scale_tile("xo_s", M)
         w2_s = scale_tile("w2_s", R)
         vs_s = scale_tile("vs_s", S)
-        ha_t = load_column("ha_t", ha)
-        sa_t = load_column("sa_t", sa)
-        sb_t = load_column("sb_t", sb)
+        xt_st = load_staged("xt_st", xt_scales, T)
+        ha_t = load_column("ha_t", ha, nc.scalar)
+        xo_st = load_staged("xo_st", xo_scales, M)
+        w2_st = load_staged("w2_st", w2_scales, R)
         ua_rows = ua.rearrange("(p t) f -> t p f", t=PACK)
         ua_t = [keep.tile([P, F], F32, name="ua_%d" % t) for t in range(PACK)]
 
-        xo_w = load_words("xo_w", xo_words[0].rearrange("p c t -> p (c t)"), U32, M)
-        xo_list = load_list("xo_list", offs3)
-        load_scales(xo_s, xo_scales, (0, 1, 2))
         nc.sync.dma_start(ua_t[0][:], ua_rows[0])
-        load_scales(xo_s, xo_scales, (3,))
-        xt_list = load_list("xt_list", offs)
         ua_list = load_list("ua_list", offs2)
-        xt_w = load_words("xt_w", xt_words[0], U16, T)
-        w2_w = load_words("w2_w", w2_words[0], U16, R)
-        load_scales(xt_s, xt_scales, (0, 1))
+        xt_list = load_list("xt_list", offs)
         nc.sync.dma_start(ua_t[1][:], ua_rows[1])
-        load_scales(xt_s, xt_scales, (2, 3))
-        load_scales(w2_s, w2_scales, (0,))
+        xo_list = load_list("xo_list", offs3)
         nc.sync.dma_start(ua_t[2][:], ua_rows[2])
-        load_scales(w2_s, w2_scales, (1, 2, 3))
+        w2_w = load_words("w2_w", w2_words[0], U16, R)
         nc.sync.dma_start(ua_t[3][:], ua_rows[3])
+        xo_w = load_words("xo_w", xo_words[0].rearrange("p c t -> p (c t)"), U32, M)
+        xt_w = load_words("xt_w", xt_words[0], U16, T)
         put_list = load_list("put_list", offs4)
         vs_w = load_words("vs_w", vs_words[0], U16, S)
         vs_list = load_list("vs_list", offs7)
         load_scales(vs_s, vs_scales, (0, 1, 2, 3))
         sb_list = load_list("sb_list", offs6)
         sa_list = load_list("sa_list", offs5)
+        sa_t = load_column("sa_t", sa, nc.sync)
+        sb_t = load_column("sb_t", sb, nc.sync)
 
         board = []
         for t in range(PACK):
@@ -99,10 +108,11 @@ def tile_picked_tokens_codes_bank_boardmixed_store_plain_kernel(
             nc.vector.memset(tile[:], 0.0)
             board.append(tile)
 
-        xo_gw = gather("xo_gw", xo_w, xo_list, U32, J)
-        xo_gs = gather("xo_gs", xo_s, xo_list, U8, J)
-        xt_gw = gather("xt_gw", xt_w, xt_list, U16, J)
+        spread(xt_s, xt_st)
+        spread(xo_s, xo_st)
         xt_gs = gather("xt_gs", xt_s, xt_list, U8, J)
+        xo_gs = gather("xo_gs", xo_s, xo_list, U8, J)
+        spread(w2_s, w2_st)
 
         w2_dw = keep.tile([P, R], U16, name="w2_dw", align_bytes=64)
         w2_ds = keep.tile([P, R], U8, name="w2_ds", align_bytes=64)
@@ -111,34 +121,56 @@ def tile_picked_tokens_codes_bank_boardmixed_store_plain_kernel(
 
         parts = [(0, 0, J // 2), (0, J // 2, J // 2)] + [(t, 0, J) for t in range(1, PACK)]
         acc = [psum.tile([P, n], F32, name="acc_%d" % i) for i, (t, j0, n) in enumerate(parts)]
-        for i, (t, j0, n) in enumerate(parts):
-            cols = slice(P * t, P * (t + 1))
-            nc.tensor.matmul_mx(acc[i][:], lhsT=w2_dw[:, cols].bitcast(FP4X4), lhsT_scale=w2_ds[:, cols],
-                                rhs=xo_gw[:, j0 : j0 + n].bitcast(FP8X4), rhs_scale=xo_gs[:, j0 : j0 + n],
-                                start=True, stop=False)
 
         wc_pair = [keep.tile([P, 2, R], BF16, name="wc_pair_%d" % u) for u in range(2)]
         for j in range(PACK):
             nc.scalar.activation(wc_pair[j // 2][:, j % 2, :], ua_t[j][:].indirect(ua_list[:]), COPY, scale=ha_t[:, j : j + 1])
         wc_grp = [keep.tile([P, P, PACK], BF16, name="wc_grp_%d" % t, align_bytes=64) for t in range(PACK)]
-        wc_w = [keep.tile([P, P], U32, name="wc_w_%d" % t, align_bytes=64) for t in range(PACK)]
-        wc_s = [keep.tile([P, P], U8, name="wc_s_%d" % t, align_bytes=64) for t in range(PACK)]
         dealt = [wc_pair[u][:].rearrange("p j (m t) -> p t m j", t=PACK) for u in range(2)]
         for t in range(PACK):
             nc.vector.tensor_copy(wc_grp[t][:, :, 0:2], dealt[0][:, t])
-        for t in range(2):
-            nc.vector.tensor_copy(wc_grp[t][:, :, 2:4], dealt[1][:, t])
-        for t in range(2, PACK):
-            nc.scalar.copy(wc_grp[t][:, :, 2:4], dealt[1][:, t])
         for t in range(PACK):
-            nc.vector.quantize_mx(wc_w[t][:].bitcast(FP8X4), wc_s[t][:], wc_grp[t][:].rearrange("p m j -> p (m j)"))
-        for i, (t, j0, n) in enumerate(parts):
-            nc.tensor.matmul_mx(acc[i][:], lhsT=wc_w[t][:].bitcast(FP8X4), lhsT_scale=wc_s[t][:],
-                                rhs=xt_gw[:, j0 : j0 + n].bitcast(FP4X4), rhs_scale=xt_gs[:, j0 : j0 + n],
-                                start=False, stop=True)
+            nc.scalar.copy(wc_grp[t][:, :, 2:4], dealt[1][:, t])
 
+        xo_gw = gather("xo_gw", xo_w, xo_list, U32, J)
+        wc_s = [keep.tile([P, P], U8, name="wc_s_%d" % t, align_bytes=64) for t in range(PACK)]
+        wc_w = [None] * PACK
+
+        def quantise(u, tag):
+            words = keep.tile([P, 2 * P], U32, name="wc_w_%d" % u, tag=tag, align_bytes=64)
+            for t in (2 * u, 2 * u + 1):
+                wc_w[t] = words[:, (t % 2) * P : (t % 2 + 1) * P]
+                nc.vector.quantize_mx(wc_w[t].bitcast(FP8X4), wc_s[t][:], wc_grp[t][:].rearrange("p m j -> p (m j)"))
+
+        quantise(0, "xo_w")
+        xt_gw = keep.tile([P, J], U16, name="xt_gw", align_bytes=64)
+        for h in range(2):
+            nc.vector.tensor_copy(xt_gw[:, h * J // 2 : (h + 1) * J // 2],
+                                  xt_w[:].indirect(xt_list[:, h * J // 2 // LIST_ROWS : (h + 1) * J // 2 // LIST_ROWS]))
+        quantise(1, "xt_w")
         vs_gw = keep.tile([P, N], U16, name="vs_gw", tag="wc_grp_3", align_bytes=64)
         nc.vector.tensor_copy(vs_gw[:], vs_w[:].indirect(vs_list[:]))
+
+        def notes_pass(i, first):
+            t, j0, n = parts[i]
+            cols = slice(P * t, P * (t + 1))
+            nc.tensor.matmul_mx(acc[i][:], lhsT=w2_dw[:, cols].bitcast(FP4X4), lhsT_scale=w2_ds[:, cols],
+                                rhs=xo_gw[:, j0 : j0 + n].bitcast(FP8X4), rhs_scale=xo_gs[:, j0 : j0 + n],
+                                start=first, stop=not first)
+
+        def tokens_pass(i, first):
+            t, j0, n = parts[i]
+            nc.tensor.matmul_mx(acc[i][:], lhsT=wc_w[t].bitcast(FP8X4), lhsT_scale=wc_s[t][:],
+                                rhs=xt_gw[:, j0 : j0 + n].bitcast(FP4X4), rhs_scale=xt_gs[:, j0 : j0 + n],
+                                start=first, stop=not first)
+
+        for i in range(3):
+            notes_pass(i, True)
+        for i in range(3):
+            tokens_pass(i, False)
+        for i in range(3, 5):
+            tokens_pass(i, True)
+            notes_pass(i, False)
 
         hidden = [keep.tile([P, n], F32, name="hidden_%d" % i, align_bytes=64) for i, (t, j0, n) in enumerate(parts)]
 

from contextlib import ExitStack

import concourse.mybir as mybir

K, J, R, T, F, Z, M, C, O, N, S = 512, 512, 512, 2048, 2048, 512, 1024, 1024, 256, 256, 1024
FLOPS = 2 * K * R * J + 2 * Z * R * J + 2 * R * N * O

F32 = mybir.dt.float32
BF16 = mybir.dt.bfloat16
I32 = mybir.dt.int32
U32 = mybir.dt.uint32
U16 = mybir.dt.uint16
U8 = mybir.dt.uint8
FP8X4 = mybir.dt.float8_e4m3fn_x4
FP4X4 = mybir.dt.float4_e2m1fn_x4
COPY = mybir.ActivationFunctionType.Copy
MAX = mybir.AluOpType.max

P = 128
PACK = 4
LIST_ROWS = 16


def tile_picked_tokens_codes_bank_boardmixed_store_plain_kernel(
    tc, xt_words, xt_scales, ua, ha, xo_words, xo_scales, w2_words, w2_scales, sa, sb, vs_words, vs_scales,
    offs, offs2, offs3, offs4, offs5, offs6, offs7, out,
):
    nc = tc.nc
    with ExitStack() as ctx:
        lists = ctx.enter_context(tc.tile_pool(name="lists", bufs=1))
        keep = ctx.enter_context(tc.tile_pool(name="keep", bufs=1))
        psum = ctx.enter_context(tc.psum_pool(name="psum", bufs=1))

        def load_list(name, src):
            tile = lists.tile([P, src.shape[1]], U16, name=name)
            nc.sync.dma_start(tile[:], src)
            return tile

        def load_words(name, src, dtype, width):
            tile = keep.tile([P, width], dtype, name=name, align_bytes=64)
            nc.sync.dma_start(tile[:].bitcast(I32), src.bitcast(I32))
            return tile

        def scale_tile(name, width):
            tile = keep.tile([P, width], U8, name=name, align_bytes=64)
            nc.vector.memset(tile[:].bitcast(I32), 0)
            return tile

        def load_scales(tile, src, quadrants):
            for q in quadrants:
                nc.sync.dma_start(tile[q:P:32, :].bitcast(I32), src[0, q:16:4, :].bitcast(I32))

        def load_staged(name, src, width):
            tile = keep.tile([P, 2, width // 4], I32, name=name)
            rows = src[0].bitcast(I32).rearrange("(h q i) w -> h i q w", h=2, q=2)
            for h in range(2):
                nc.scalar.dma_start(tile[64 * h : 64 * h + 4], rows[h])
            return tile

        def spread(tile, staged):
            for q in range(4):
                h = q // 2
                nc.vector.tensor_copy(tile[32 * q : 32 * q + 4, :].bitcast(I32), staged[64 * h : 64 * h + 4, q % 2, :])

        def load_column(name, src, queue):
            tile = keep.tile([P, PACK], F32, name=name)
            queue.dma_start(tile[:], src.rearrange("(p t) o -> p (t o)", t=PACK))
            return tile

        def gather(name, window, offsets, dtype, count):
            tile = keep.tile([P, count], dtype, name=name, align_bytes=64)
            nc.vector.tensor_copy(tile[:], window[:].indirect(offsets[:]))
            return tile

        xt_s = scale_tile("xt_s", T)
        xo_s = scale_tile("xo_s", M)
        w2_s = scale_tile("w2_s", R)
        vs_s = scale_tile("vs_s", S)
        xt_st = load_staged("xt_st", xt_scales, T)
        ha_t = load_column("ha_t", ha, nc.scalar)
        xo_st = load_staged("xo_st", xo_scales, M)
        w2_st = load_staged("w2_st", w2_scales, R)
        ua_rows = ua.rearrange("(p t) f -> t p f", t=PACK)
        ua_t = [keep.tile([P, F], F32, name="ua_%d" % t) for t in range(PACK)]

        nc.sync.dma_start(ua_t[0][:], ua_rows[0])
        ua_list = load_list("ua_list", offs2)
        xt_list = load_list("xt_list", offs)
        nc.sync.dma_start(ua_t[1][:], ua_rows[1])
        xo_list = load_list("xo_list", offs3)
        nc.sync.dma_start(ua_t[2][:], ua_rows[2])
        w2_w = load_words("w2_w", w2_words[0], U16, R)
        nc.sync.dma_start(ua_t[3][:], ua_rows[3])
        xo_w = load_words("xo_w", xo_words[0].rearrange("p c t -> p (c t)"), U32, M)
        xt_w = load_words("xt_w", xt_words[0], U16, T)
        put_list = load_list("put_list", offs4)
        vs_w = load_words("vs_w", vs_words[0], U16, S)
        vs_list = load_list("vs_list", offs7)
        load_scales(vs_s, vs_scales, (0, 1, 2, 3))
        sb_list = load_list("sb_list", offs6)
        sa_list = load_list("sa_list", offs5)
        sa_t = load_column("sa_t", sa, nc.sync)
        sb_t = load_column("sb_t", sb, nc.sync)

        board = []
        for t in range(PACK):
            tile = keep.tile([P, C], F32, name="board_%d" % t)
            nc.vector.memset(tile[:], 0.0)
            board.append(tile)

        spread(xt_s, xt_st)
        spread(xo_s, xo_st)
        xt_gs = gather("xt_gs", xt_s, xt_list, U8, J)
        xo_gs = gather("xo_gs", xo_s, xo_list, U8, J)
        spread(w2_s, w2_st)

        w2_dw = keep.tile([P, R], U16, name="w2_dw", align_bytes=64)
        w2_ds = keep.tile([P, R], U8, name="w2_ds", align_bytes=64)
        nc.scalar.copy(w2_dw[:].rearrange("p (t m) -> p t m", t=PACK), w2_w[:].rearrange("p (m t) -> p t m", t=PACK))
        nc.vector.tensor_copy(w2_ds[:].rearrange("p (t m) -> p t m", t=PACK), w2_s[:].rearrange("p (m t) -> p t m", t=PACK))

        parts = [(0, 0, J // 2), (0, J // 2, J // 2)] + [(t, 0, J) for t in range(1, PACK)]
        acc = [psum.tile([P, n], F32, name="acc_%d" % i) for i, (t, j0, n) in enumerate(parts)]

        wc_pair = [keep.tile([P, 2, R], BF16, name="wc_pair_%d" % u) for u in range(2)]
        for j in range(PACK):
            nc.scalar.activation(wc_pair[j // 2][:, j % 2, :], ua_t[j][:].indirect(ua_list[:]), COPY, scale=ha_t[:, j : j + 1])
        wc_grp = [keep.tile([P, P, PACK], BF16, name="wc_grp_%d" % t, align_bytes=64) for t in range(PACK)]
        dealt = [wc_pair[u][:].rearrange("p j (m t) -> p t m j", t=PACK) for u in range(2)]
        for t in range(PACK):
            nc.vector.tensor_copy(wc_grp[t][:, :, 0:2], dealt[0][:, t])
        for t in range(PACK):
            nc.scalar.copy(wc_grp[t][:, :, 2:4], dealt[1][:, t])

        xo_gw = gather("xo_gw", xo_w, xo_list, U32, J)
        wc_s = [keep.tile([P, P], U8, name="wc_s_%d" % t, align_bytes=64) for t in range(PACK)]
        wc_w = [None] * PACK

        def quantise(u, tag):
            words = keep.tile([P, 2 * P], U32, name="wc_w_%d" % u, tag=tag, align_bytes=64)
            for t in (2 * u, 2 * u + 1):
                wc_w[t] = words[:, (t % 2) * P : (t % 2 + 1) * P]
                nc.vector.quantize_mx(wc_w[t].bitcast(FP8X4), wc_s[t][:], wc_grp[t][:].rearrange("p m j -> p (m j)"))

        quantise(0, "xo_w")
        xt_gw = keep.tile([P, J], U16, name="xt_gw", align_bytes=64)
        for h in range(2):
            nc.vector.tensor_copy(xt_gw[:, h * J // 2 : (h + 1) * J // 2],
                                  xt_w[:].indirect(xt_list[:, h * J // 2 // LIST_ROWS : (h + 1) * J // 2 // LIST_ROWS]))
        quantise(1, "xt_w")
        vs_gw = keep.tile([P, N], U16, name="vs_gw", tag="wc_grp_3", align_bytes=64)
        nc.vector.tensor_copy(vs_gw[:], vs_w[:].indirect(vs_list[:]))

        def notes_pass(i, first):
            t, j0, n = parts[i]
            cols = slice(P * t, P * (t + 1))
            nc.tensor.matmul_mx(acc[i][:], lhsT=w2_dw[:, cols].bitcast(FP4X4), lhsT_scale=w2_ds[:, cols],
                                rhs=xo_gw[:, j0 : j0 + n].bitcast(FP8X4), rhs_scale=xo_gs[:, j0 : j0 + n],
                                start=first, stop=not first)

        def tokens_pass(i, first):
            t, j0, n = parts[i]
            nc.tensor.matmul_mx(acc[i][:], lhsT=wc_w[t].bitcast(FP8X4), lhsT_scale=wc_s[t][:],
                                rhs=xt_gw[:, j0 : j0 + n].bitcast(FP4X4), rhs_scale=xt_gs[:, j0 : j0 + n],
                                start=first, stop=not first)

        for i in range(3):
            notes_pass(i, True)
        for i in range(3):
            tokens_pass(i, False)
        for i in range(3, 5):
            tokens_pass(i, True)
            notes_pass(i, False)

        hidden = [keep.tile([P, n], F32, name="hidden_%d" % i, align_bytes=64) for i, (t, j0, n) in enumerate(parts)]

        def leave(i):
            nc.scalar.copy(hidden[i][:], acc[i][:])

        def put(engine, i, first, count):
            t, j0, n = parts[i]
            window = board[t][:].indirect(put_list[:, (j0 + first) // LIST_ROWS : (j0 + first + count) // LIST_ROWS])
            if engine == "vector":
                nc.vector.tensor_copy(window, hidden[i][:, first : first + count])
            else:
                nc.scalar.activation(window, hidden[i][:, first : first + count], COPY)

        SHARE = 128
        for i in range(4):
            leave(i)
        put("vector", 0, 0, J // 2)
        put("vector", 1, 0, J // 2)
        put("scalar", 2, 0, J // 2)
        put("scalar", 2, J // 2, J // 2)
        put("vector", 3, 0, J)
        leave(4)
        put("scalar", 4, 0, SHARE)
        put("vector", 4, SHARE, J - SHARE)

        H = O // 2
        early = keep.tile([P, 2, 2, O], F32, name="early", tag="hidden_2", align_bytes=64)
        late_sb = keep.tile([P, 2, O], F32, name="late_sb")
        late_sa = [keep.tile([P, 2, H], F32, name="late_sa_%d" % h) for h in range(2)]
        hid_grp = [keep.tile([P, H, PACK], BF16, name="hid_grp_%d" % h, align_bytes=64) for h in range(2)]

        def fetch(dst, t, offsets, weight):
            nc.scalar.activation(dst, board[t][:].indirect(offsets), COPY, scale=weight[:, t : t + 1])

        def larger(h, pair, by_sa, by_sb):
            nc.vector.tensor_tensor(hid_grp[h][:, :, 2 * pair : 2 * pair + 2], by_sa.rearrange("p t o -> p o t"),
                                    by_sb.rearrange("p t o -> p o t"), MAX)

        for t in (1, 0):
            fetch(early[:, 0, t, :], t, sa_list[:], sa_t)
            fetch(early[:, 1, t, :], t, sb_list[:], sb_t)
        for h in range(2):
            larger(h, 0, early[:, 0, :, h * H : (h + 1) * H], early[:, 1, :, h * H : (h + 1) * H])
        vs_gs = keep.tile([P, N], U8, name="vs_gs", tag="hidden_4", align_bytes=64)
        nc.vector.tensor_copy(vs_gs[:], vs_s[:].indirect(vs_list[:]))
        for t in (2, 3):
            fetch(late_sb[:, t - 2, :], t, sb_list[:], sb_t)
            for h in range(2):
                fetch(late_sa[h][:, t - 2, :], t, sa_list[:, h * H // LIST_ROWS : (h + 1) * H // LIST_ROWS], sa_t)
        for h in range(2):
            larger(h, 1, late_sa[h][:], late_sb[:, :, h * H : (h + 1) * H])

        out_rows = out.rearrange("(u p) o -> p u o", p=P)
        for h in range(2):
            hid_w = keep.tile([P, H], U32, name="hid_w_%d" % h, align_bytes=64)
            hid_s = keep.tile([P, H], U8, name="hid_s_%d" % h, align_bytes=64)
            nc.vector.quantize_mx(hid_w[:].bitcast(FP8X4), hid_s[:], hid_grp[h][:].rearrange("p o t -> p (o t)"))
            res = psum.tile([P, N // P, H], F32, name="res_%d" % h)
            for u in range(N // P):
                cols = slice(P * u, P * (u + 1))
                nc.tensor.matmul_mx(res[:, u, :], lhsT=vs_gw[:, cols].bitcast(FP4X4), lhsT_scale=vs_gs[:, cols],
                                    rhs=hid_w[:].bitcast(FP8X4), rhs_scale=hid_s[:], start=True, stop=True)
            staged = keep.tile([P, N // P, H], F32, name="staged_%d" % h)
            if h == 0:
                nc.scalar.copy(staged[:], res[:])
                nc.scalar.dma_start(out_rows[:, :, h * H : (h + 1) * H], staged[:])
            else:
                nc.vector.tensor_copy(staged[:], res[:])
                nc.sync.dma_start(out_rows[:, :, h * H : (h + 1) * H], staged[:])
